import numpy as np, ml_dtypes
CORES = [24,25,26,27,48,49,50,51,72,73,74,75,96,97,98,99]
N = 16
TOK, CAP, FF = 512, 48, 4
def entries(a): return a.T.reshape(-1)
def pack(v, P): return np.ascontiguousarray(np.asarray(v, np.int32).reshape(-1, P).T)
def lists(rng, how):
    E = rng.integers(0, N, (N, TOK))
    if how == "hot": E[:] = rng.integers(N)
    if how == "none": E = (int(rng.integers(N)) + 1 + rng.integers(0, N - 1, (N, TOK))) % N
    if how == "skew": E = np.where(rng.random((N, TOK)) < 0.7, rng.integers(0, N, (N, 1)), E)
    if how == "even": E = np.stack([rng.permutation(np.arange(TOK) % N) for r in range(N)])
    if how == "own": E = np.repeat(np.arange(N).reshape(N, 1), TOK, axis=1)
    return {"ex": np.stack([pack(E[r], 16) for r in range(N)]), "pos": np.stack([pack(p, 16) for p in np.stack([np.array([np.sum(E[r, :t] == E[r, t]) for t in range(TOK)]) for r in range(N)])])}
def setup_inputs(rng):
    return dict({"x": rng.standard_normal((N, 128, TOK), dtype=np.float32).astype(ml_dtypes.bfloat16), "w1": (rng.standard_normal((N, 128, FF * 128), dtype=np.float32) / 8).astype(ml_dtypes.bfloat16), "w2": (rng.standard_normal((N, 128, FF * 128), dtype=np.float32) / 16).astype(ml_dtypes.bfloat16)}, **lists(rng, "uniform"))
def setup_inputs_even(rng):
    d = setup_inputs(rng); d.update(lists(rng, "even"))
    for k in ("x",): d[k] = (d[k].astype(np.float32) * 1024.0).astype(d[k].dtype)
    return d
def setup_inputs_hot(rng):
    d = setup_inputs(rng); d.update(lists(rng, "hot"))
    for k in ("x",): d[k] = (d[k].astype(np.float32) * (1 / 1024.0)).astype(d[k].dtype)
    return d
def setup_inputs_none(rng):
    d = setup_inputs(rng); d.update(lists(rng, "none"))
    return d
def setup_inputs_own(rng):
    d = setup_inputs(rng); d.update(lists(rng, "own"))
    return d
def setup_inputs_skew(rng):
    d = setup_inputs(rng); d.update(lists(rng, "skew"))
    return d
def check_inputs(x):
    bad = []
    if x["ex"].min() < 0 or x["ex"].max() >= N: bad.append("ex out of range")
    E = np.stack([entries(a) for a in x["ex"]])
    if not np.array_equal(np.stack([entries(a) for a in x["pos"]]), np.stack([np.array([np.sum(E[r, :t] == E[r, t]) for t in range(TOK)]) for r in range(N)])): bad.append("pos isn't the place")
    return bad
def reference(x, w1, w2, ex, pos):
    X, W1, W2 = x.astype(np.float64), w1.astype(np.float64), w2.astype(np.float64)
    y = np.zeros((N, 128, TOK))
    for r in range(N):
        E = entries(ex[r]); place = np.array([np.sum(E[:t] == E[t]) for t in range(TOK)])
        for k in range(N):
            m = (E == k) & (place < CAP)
            y[r][:, m] = sum(W2[k][:, 128 * f:128 * f + 128].T @ np.maximum(W1[k][:, 128 * f:128 * f + 128].T @ X[r][:, m], 0.0) for f in range(FF))
    return {"y": y.astype(ml_dtypes.bfloat16)}

@@ -1,0 +1,258 @@
+from concourse.bass import DstId, RemoteDMATransfer
+from concourse.mybir import AluOpType, ActivationFunctionType
+
+TOK, CAP, FF = 512, 48, 4
+NE = 4
+GRP = NE * CAP
+SLOTS = 16 * CAP
+WIN = SLOTS + 128 + 16 * 31
+DROP = 8192.0
+P1_ENG, FWD_ENG, OFF_ENG, DIR_ENG, W_ENG = 4, 4, 8, 2, 8
+RET_DIRECT = False
+
+SCRATCH = {
+    "idx": ("sbuf", [128, 64], "int32"),
+    "ai": ("sbuf", [128, 32], "int32"),
+    "fl": ("sbuf", [128, 128], "float32"),
+    "rep": ("sbuf", [128, 512], "float32"),
+    "q": ("sbuf", [128, 32], "float32"),
+    "zs": ("sbuf", [128, 32], "float32"),
+    "offs": ("sbuf", [128, 32], "uint16"),
+    "offg": ("sbuf", [128, 32], "uint16"),
+    "xs": ("sbuf", [128, TOK], "bfloat16"),
+    "ys": ("sbuf", [128, TOK], "bfloat16"),
+    "S": ("sbuf", [128, WIN], "bfloat16"),
+    "R": ("sbuf", [128, SLOTS + 8], "bfloat16"),
+    "w1s": ("sbuf", [128, FF * 128], "bfloat16"),
+    "w2s": ("sbuf", [128, FF * 128], "bfloat16"),
+    "L": ("sbuf", [128, NE, 4, CAP], "bfloat16"),
+    "M": ("sbuf", [128, 4, NE, CAP], "bfloat16"),
+    "V": ("sbuf", [128, 4 * GRP], "bfloat16"),
+    "h": ("sbuf", [128, 2 * FF * GRP], "bfloat16"),
+    "OB": ("sbuf", [128, 4 * GRP], "bfloat16"),
+    "RL": ("sbuf", [128, 4 * GRP], "bfloat16"),
+    "hp0": ("psum", [128, 512], "float32"),
+    "hp1": ("psum", [128, 512], "float32"),
+    "hp2": ("psum", [128, 512], "float32"),
+    "hp3": ("psum", [128, 512], "float32"),
+    "op0": ("psum", [128, 512], "float32"),
+    "op1": ("psum", [128, 512], "float32"),
+    "zp": ("psum", [128, 512], "float32"),
+}
+SEMAPHORES = ["s_idx", "s_x0", "s_x1", "s_w", "s_ws", "s_rep", "s_set", "s_g", "s_d2", "s_f", "s_z", "s_zs", "s_off",
+              "s_sc", "s_og", "s_m", "s_ml", "s_l1", "s_l2", "s_ra", "s_rv", "s_o", "s_self", "s_gv", "s_ga", "s_y",
+              "lsem", "r2"] + ["p1_%d" % i for i in range(4)] + ["p2_%d" % i for i in range(4)] + \
+             ["r1_%d" % i for i in range(4)]
+
+
+def plan(T, topo):
+    cores = list(T.cores)
+    chips = sorted(set(topo.chip(c) for c in cores))
+    n = len(chips)
+    rc = [[c for c in cores if topo.chip(c) == ch] for ch in chips]
+    everyone = range(topo.CORES_PER_CHIP * topo.CHIPS)
+    host, part = [], []
+    for i, ch in enumerate(chips):
+        far = [c for c in cores if topo.chip(c) != ch and not topo.same_plane(ch, topo.chip(c))]
+        mine = [c for c in everyone if topo.chip(c) == ch]
+        port = [c for c in mine if all(topo.may_write(c, d) for d in far)]
+        free_port = [c for c in port if c not in rc[i]]
+        free_rest = [c for c in mine if c not in port and c not in rc[i]]
+        host.append([c if c in port else free_port.pop(0) for c in rc[i]])
+        part.append([c if c not in port else free_rest.pop(0) for c in rc[i]])
+    plane = [[b for b in range(n) if b != a and topo.same_plane(chips[a], chips[b])] for a in range(n)]
+    cross = [sorted([b for b in range(n) if b != a and b not in plane[a]], key=lambda b, a=a: (b - a) % n)
+             for a in range(n)]
+    take = [sorted(cross[x], key=lambda a, x=x: (cross[a].index(x), (x - a) % n)) for x in range(n)]
+    back = [sorted(cross[a], key=lambda x, a=a: (take[x].index(a), (x - a) % n)) + plane[a] for a in range(n)]
+    return dict(chips=chips, rc=rc, host=host, part=part, plane=plane, cross=cross, take=take, back=back)
+
+
+def rank_program(g, core, T, topo):
+    P = plan(T, topo)
+    if topo.chip(core) not in P["chips"]:
+        return
+    ci = P["chips"].index(topo.chip(core))
+    rc, host, part = P["rc"], P["host"], P["part"]
+    is_rank, is_host, is_part = core in rc[ci], core in host[ci], core in part[ci]
+    if not (is_rank or is_host or is_part):
+        return
+    sem, ve, se, te, sy = T.sem, g.vector, g.scalar, g.tensor, g.sync
+    Alu, Act = AluOpType, ActivationFunctionType
+    me = rc[ci].index(core) if is_rank else None
+    ex = host[ci].index(core) if is_host else part[ci].index(core)
+    sent = [0]
+
+    def engines(dst, lo, cnt):
+        m = topo.mask(core, dst)
+        bits = [b for b in range(m.bit_length()) if (m >> b) & 1]
+        return sum(1 << b for b in bits[lo:lo + cnt])
+
+    def tr(dst, out, in_, rsem, lo, cnt):
+        rid, pid, _ = topo.addr(dst)
+        sent[0] += cnt
+        return RemoteDMATransfer(dst_ids=[DstId(rid=rid, pnc=pid)], dma_engine_mask=engines(dst, lo, cnt),
+                                 remote_sem=rsem, src=in_, dst=out)
+
+    def send(dst, out, in_, rsem, cnt):
+        rid, pid, _ = topo.addr(dst)
+        sent[0] += cnt
+        g.remote_dma(out, in_, rsem, sem.lsem, pid, rid, engines(dst, 0, cnt))
+
+    if is_rank:
+        sy.dma_start(T.idx[0:16, 0:32], T.ex[:, :]).then_inc(sem.s_idx, 16)
+        se.dma_start(T.idx[0:16, 32:64], T.pos[:, :]).then_inc(sem.s_idx, 16)
+        sy.dma_start(T.xs[:, 0:256], T.x[:, 0:256]).then_inc(sem.s_x0, 16)
+        se.dma_start(T.xs[:, 256:512], T.x[:, 256:512]).then_inc(sem.s_x1, 16)
+        sy.dma_start(T.w1s[:, :], T.w1[:, :]).then_inc(sem.s_w, 16)
+        se.dma_start(T.w2s[:, :], T.w2[:, :]).then_inc(sem.s_w, 16)
+        for i, coef in enumerate((12.0, 1.0, 180.0, DROP)):
+            ve.memset(T.rep[0:16, 128 * i:128 * i + 128], coef).then_inc(sem.s_rep, 1)
+        ve.memset(T.S[:, 0:SLOTS], 0.0).then_inc(sem.s_set, 1)
+        ve.memset(T.R[:, SLOTS:SLOTS + 8], 0.0).then_inc(sem.s_set, 1)
+        g.wait_ge(sem.s_rep, 4)
+        g.affine_select(T.rep[0:16, :], T.rep[0:16, :], [[0, 32], [-1, 16]], Alu.is_equal, 0.0, 0, 1).then_inc(sem.s_g, 1)
+        g.iota(T.q[:, :], [[16, 32]], SLOTS, 1, allow_small_or_imprecise_dtypes=True).then_inc(sem.s_g, 1)
+        ve.wait_ge(sem.s_idx, 32)
+        ve.tensor_scalar(T.ai[0:16, :], T.idx[0:16, 0:32], 3, None, Alu.bitwise_and).then_inc(sem.s_d2, 1)
+        ve.tensor_copy(T.fl[0:16, 0:64], T.idx[0:16, 0:64]).then_inc(sem.s_f, 1)
+        ve.tensor_scalar(T.fl[0:16, 96:128], T.idx[0:16, 32:64], CAP, None, Alu.is_ge).then_inc(sem.s_f, 1)
+        ve.wait_ge(sem.s_d2, 1)
+        ve.tensor_copy(T.fl[0:16, 64:96], T.ai[0:16, :]).then_inc(sem.s_f, 1)
+        te.wait_ge(sem.s_g, 2)
+        te.wait_ge(sem.s_f, 3)
+        for i in range(4):
+            mm = te.matmul(T.zp[:, 0:32], T.rep[0:16, 128 * i:128 * i + 128], T.fl[0:16, 32 * i:32 * i + 32], i == 0, i == 3)
+        mm.then_inc(sem.s_z, 1)
+        ve.wait_ge(sem.s_z, 1)
+        ve.wait_ge(sem.s_g, 2)
+        ve.tensor_tensor(T.zs[:, :], T.zp[:, 0:32], T.q[:, :], Alu.min).then_inc(sem.s_zs, 1)
+        ve.wait_ge(sem.s_zs, 1)
+        ve.tensor_copy(T.offs[:, :], T.zs[:, :]).then_inc(sem.s_off, 1)
+        ve.wait_ge(sem.s_off, 1)
+        ve.wait_ge(sem.s_set, 2)
+        ve.wait_ge(sem.s_x0, 16)
+        ve.tensor_copy(T.S[:, 0:WIN].indirect(T.offs[:, 0:16]), T.xs[:, 0:256]).then_inc(sem.s_sc, 1)
+        ve.wait_ge(sem.s_x1, 16)
+        ve.wait_ge(sem.s_sc, 1)
+        ve.tensor_copy(T.S[:, 0:WIN].indirect(T.offs[:, 16:32]), T.xs[:, 256:512]).then_inc(sem.s_sc, 1)
+        ve.tensor_scalar(T.offg[:, :], T.zp[:, 0:32], float(SLOTS), None, Alu.min).then_inc(sem.s_og, 1)
+        g.wait_ge(sem.s_sc, 2)
+        g.remote_dma_fused([tr(host[ci][e], T.L[:, me, :, :], T.S[:, GRP * e:GRP * e + GRP], sem["p1_%d" % me],
+                               P1_ENG * e, P1_ENG) for e in range(NE) if host[ci][e] != core], local_sem=sem.lsem)
+        other = part[ci][me] if is_host else host[ci][me]
+        g.wait_ge(sem.s_w, 32)
+        g.remote_dma_fused([tr(other, T.w1s[:, :], T.w1s[:, :], sem.s_ws, 0, W_ENG),
+                            tr(other, T.w2s[:, :], T.w2s[:, :], sem.s_ws, W_ENG, W_ENG)], local_sem=sem.lsem)
+
+    n_m = n_ml = 0
+    if is_host:
+        if is_rank:
+            ve.wait_ge(sem.s_sc, 2)
+            for c in range(4):
+                src = T.S[:, GRP * ex + CAP * c:GRP * ex + CAP * c + CAP]
+                out = T.V[:, GRP * ci + CAP * me:GRP * ci + CAP * me + CAP] if c == ci else T.M[:, c, me, :]
+                ve.tensor_copy(out, src).then_inc(sem.s_m, 1)
+                n_m += 1
+        for s in range(NE):
+            if rc[ci][s] == core:
+                continue
+            ve.wait_ge(sem["p1_%d" % s], P1_ENG)
+            ve.tensor_copy(T.M[:, :, s, :], T.L[:, s, :, :]).then_inc(sem.s_m, 1)
+            n_m += 1
+            se.wait_ge(sem["p1_%d" % s], P1_ENG)
+            se.activation(T.V[:, GRP * ci + CAP * s:GRP * ci + CAP * s + CAP], T.L[:, s, ci, :], Act.Copy).then_inc(sem.s_ml, 1)
+            n_ml += 1
+        g.wait_ge(sem.s_m, n_m)
+        for c in P["cross"][ci] + P["plane"][ci]:
+            dst = host[c][ex] if c in P["cross"][ci] else part[c][ex]
+            send(dst, T.V[:, GRP * ci:GRP * ci + GRP], T.M[:, c, :, :], sem["p2_%d" % ci], OFF_ENG)
+
+    if is_host:
+        groups = [(ci, [(sem.s_m, n_m), (sem.s_ml, n_ml)])] + [(a, [(sem["p2_%d" % a], OFF_ENG)]) for a in P["take"][ci]]
+    else:
+        groups = [(a, [(sem["p2_%d" % a], OFF_ENG)]) for a in P["plane"][ci]]
+    if is_rank:
+        te.wait_ge(sem.s_w, 32)
+    else:
+        te.wait_ge(sem.s_ws, 2 * W_ENG)
+    hp = [T.hp0, T.hp1, T.hp2, T.hp3]
+    op = [T.op0, T.op1]
+    for n, (c, waits) in enumerate(groups):
+        for s_, v_ in waits:
+            te.wait_ge(s_, v_)
+        for f in range(FF):
+            te.matmul(hp[f][:, 0:GRP], T.w1s[:, 128 * f:128 * f + 128], T.V[:, GRP * c:GRP * c + GRP], True, True).then_inc(sem.s_l1, 1)
+        for f in range(FF):
+            hb = T.h[:, ((n % 2) * FF + f) * GRP:((n % 2) * FF + f) * GRP + GRP]
+            eng = se if f % 2 == 0 else ve
+            eng.wait_ge(sem.s_l1, FF * n + f + 1)
+            if n >= 2:
+                eng.wait_ge(sem.s_l2, FF * (n - 2) + f + 1)
+            if f % 2 == 0:
+                se.activation(hb, hp[f][:, 0:GRP], Act.Relu).then_inc(sem.s_ra, 1)
+            else:
+                ve.tensor_scalar(hb, hp[f][:, 0:GRP], 0.0, None, Alu.max).then_inc(sem.s_rv, 1)
+        if n >= 2:
+            te.wait_ge(sem.s_o, n - 1)
+        for f in range(FF):
+            hb = T.h[:, ((n % 2) * FF + f) * GRP:((n % 2) * FF + f) * GRP + GRP]
+            te.wait_ge(sem.s_ra if f % 2 == 0 else sem.s_rv, 2 * n + f // 2 + 1)
+            te.matmul(op[n % 2][:, 0:GRP], T.w2s[:, 128 * f:128 * f + 128], hb, f == 0, f == FF - 1).then_inc(sem.s_l2, 1)
+        ve.wait_ge(sem.s_l2, FF * n + FF)
+        ve.tensor_copy(T.OB[:, GRP * c:GRP * c + GRP], op[n % 2][:, 0:GRP]).then_inc(sem.s_o, 1)
+
+    def rcol(e, x):
+        return GRP * e + CAP * x
+
+    n_self = 0
+
+    def forward(buf, x):
+        g.remote_dma_fused([tr(rc[ci][s], T.R[:, rcol(ex, x):rcol(ex, x) + CAP], buf[:, GRP * x + CAP * s:GRP * x + CAP * s + CAP],
+                               sem.r2, FWD_ENG * s, FWD_ENG) for s in range(NE) if rc[ci][s] != core], local_sem=sem.lsem)
+
+    for n, (c, _) in enumerate(groups):
+        g.wait_ge(sem.s_o, n + 1)
+        if c == ci:
+            forward(T.OB, ci)
+            if is_rank:
+                ve.wait_ge(sem.s_o, len(groups))
+                ve.tensor_copy(T.R[:, rcol(ex, ci):rcol(ex, ci) + CAP], T.OB[:, GRP * ci + CAP * me:GRP * ci + CAP * me + CAP]).then_inc(sem.s_self, 1)
+                n_self += 1
+        elif RET_DIRECT:
+            g.remote_dma_fused([tr(rc[c][s], T.R[:, rcol(ex, ci):rcol(ex, ci) + CAP], T.OB[:, GRP * c + CAP * s:GRP * c + CAP * s + CAP],
+                                   sem.r2, DIR_ENG * s, DIR_ENG) for s in range(NE)], local_sem=sem.lsem)
+        else:
+            send(host[c][ex], T.RL[:, GRP * ci:GRP * ci + GRP], T.OB[:, GRP * c:GRP * c + GRP], sem["r1_%d" % ci], OFF_ENG)
+    if is_host and not RET_DIRECT:
+        for x in P["back"][ci]:
+            g.wait_ge(sem["r1_%d" % x], OFF_ENG)
+            forward(T.RL, x)
+            if is_rank:
+                ve.wait_ge(sem["r1_%d" % x], OFF_ENG)
+                ve.tensor_copy(T.R[:, rcol(ex, x):rcol(ex, x) + CAP], T.RL[:, GRP * x + CAP * me:GRP * x + CAP * me + CAP]).then_inc(sem.s_self, 1)
+                n_self += 1
+
+    if is_rank:
+        total = 0
+        for e in range(NE):
+            for x in range(4):
+                if x == ci or not RET_DIRECT:
+                    total += 0 if host[ci][e] == core else FWD_ENG
+                else:
+                    total += DIR_ENG
+        for eng in (ve, se):
+            eng.wait_ge(sem.r2, total)
+            if n_self:
+                eng.wait_ge(sem.s_self, n_self)
+            eng.wait_ge(sem.s_og, 1)
+            eng.wait_ge(sem.s_set, 2)
+        ve.tensor_copy(T.ys[:, 0:256], T.R[:, 0:SLOTS + 8].indirect(T.offg[:, 0:16])).then_inc(sem.s_gv, 1)
+        se.activation(T.ys[:, 256:512], T.R[:, 0:SLOTS + 8].indirect(T.offg[:, 16:32]), Act.Copy).then_inc(sem.s_ga, 1)
+        sy.wait_ge(sem.s_gv, 1)
+        sy.dma_start(T.y[:, 0:256], T.ys[:, 0:256]).then_inc(sem.s_y, 16)
+        se.wait_ge(sem.s_ga, 1)
+        se.dma_start(T.y[:, 256:512], T.ys[:, 256:512]).then_inc(sem.s_y, 16)
+        sy.wait_ge(sem.s_y, 32)
+    if sent[0]:
+        g.wait_ge(sem.lsem, sent[0])

@@ -7,14 +7,17 @@ GRP = NE * CAP
 SLOTS = 16 * CAP
 WIN = SLOTS + 128 + 16 * 31
 DROP = 8192.0
-P1_ENG, FWD_ENG, OFF_ENG, DIR_ENG, W_ENG = 4, 4, 8, 2, 8
-RET_DIRECT = False
+P1_ENG, FWD_ENG, OFF_ENG = 4, 4, 8
+WA = 128
+WR = (2 * FF * 128 - WA) // 2
 
 SCRATCH = {
     "idx": ("sbuf", [128, 64], "int32"),
     "ai": ("sbuf", [128, 32], "int32"),
-    "fl": ("sbuf", [128, 128], "float32"),
-    "rep": ("sbuf", [128, 512], "float32"),
+    "fl": ("sbuf", [128, 32], "float32"),
+    "flb": ("sbuf", [128, 96], "bfloat16"),
+    "rep": ("sbuf", [128, 128], "float32"),
+    "repb": ("sbuf", [128, 384], "bfloat16"),
     "q": ("sbuf", [128, 32], "float32"),
     "zs": ("sbuf", [128, 32], "float32"),
     "offs": ("sbuf", [128, 32], "uint16"),
@@ -23,8 +26,7 @@ SCRATCH = {
     "ys": ("sbuf", [128, TOK], "bfloat16"),
     "S": ("sbuf", [128, WIN], "bfloat16"),
     "R": ("sbuf", [128, SLOTS + 8], "bfloat16"),
-    "w1s": ("sbuf", [128, FF * 128], "bfloat16"),
-    "w2s": ("sbuf", [128, FF * 128], "bfloat16"),
+    "W": ("sbuf", [128, 2 * FF * 128], "bfloat16"),
     "L": ("sbuf", [128, NE, 4, CAP], "bfloat16"),
     "M": ("sbuf", [128, 4, NE, CAP], "bfloat16"),
     "V": ("sbuf", [128, 4 * GRP], "bfloat16"),
@@ -39,9 +41,9 @@ SCRATCH = {
     "op1": ("psum", [128, 512], "float32"),
     "zp": ("psum", [128, 512], "float32"),
 }
-SEMAPHORES = ["s_idx", "s_x0", "s_x1", "s_w", "s_ws", "s_rep", "s_set", "s_g", "s_d2", "s_f", "s_z", "s_zs", "s_off",
-              "s_sc", "s_og", "s_m", "s_ml", "s_l1", "s_l2", "s_ra", "s_rv", "s_o", "s_self", "s_gv", "s_ga", "s_y",
-              "lsem", "r2"] + ["p1_%d" % i for i in range(4)] + ["p2_%d" % i for i in range(4)] + \
+SEMAPHORES = ["s_idx", "s_x0", "s_x1", "s_wa", "s_w", "s_ws", "s_cf", "s_and", "s_set", "s_g", "s_f", "s_z",
+              "s_zs", "s_off", "s_sc", "s_og", "s_m", "s_ml", "s_l1", "s_l2", "s_ra", "s_rv", "s_o", "s_self", "s_gv",
+              "s_ga", "s_y", "lsem", "r2"] + ["p1_%d" % i for i in range(4)] + ["p2_%d" % i for i in range(4)] + \
              ["r1_%d" % i for i in range(4)]
 
 
@@ -83,67 +85,78 @@ def rank_program(g, core, T, topo):
     ex = host[ci].index(core) if is_host else part[ci].index(core)
     sent = [0]
 
-    def engines(dst, lo, cnt):
-        m = topo.mask(core, dst)
-        bits = [b for b in range(m.bit_length()) if (m >> b) & 1]
-        return sum(1 << b for b in bits[lo:lo + cnt])
+    def bits(dst, src=core):
+        m = topo.mask(src, dst)
+        return [b for b in range(m.bit_length()) if (m >> b) & 1]
 
-    def tr(dst, out, in_, rsem, lo, cnt):
+    def tr(dst, out, in_, rsem, eng):
         rid, pid, _ = topo.addr(dst)
-        sent[0] += cnt
-        return RemoteDMATransfer(dst_ids=[DstId(rid=rid, pnc=pid)], dma_engine_mask=engines(dst, lo, cnt),
+        sent[0] += len(eng)
+        return RemoteDMATransfer(dst_ids=[DstId(rid=rid, pnc=pid)], dma_engine_mask=sum(1 << b for b in eng),
                                  remote_sem=rsem, src=in_, dst=out)
 
-    def send(dst, out, in_, rsem, cnt):
+    def send(dst, out, in_, rsem, eng):
         rid, pid, _ = topo.addr(dst)
-        sent[0] += cnt
-        g.remote_dma(out, in_, rsem, sem.lsem, pid, rid, engines(dst, 0, cnt))
+        sent[0] += len(eng)
+        g.remote_dma(out, in_, rsem, sem.lsem, pid, rid, sum(1 << b for b in eng))
 
     if is_rank:
+        other = part[ci][me] if is_host else host[ci][me]
         sy.dma_start(T.idx[0:16, 0:32], T.ex[:, :]).then_inc(sem.s_idx, 16)
         se.dma_start(T.idx[0:16, 32:64], T.pos[:, :]).then_inc(sem.s_idx, 16)
         sy.dma_start(T.xs[:, 0:256], T.x[:, 0:256]).then_inc(sem.s_x0, 16)
         se.dma_start(T.xs[:, 256:512], T.x[:, 256:512]).then_inc(sem.s_x1, 16)
-        sy.dma_start(T.w1s[:, :], T.w1[:, :]).then_inc(sem.s_w, 16)
-        se.dma_start(T.w2s[:, :], T.w2[:, :]).then_inc(sem.s_w, 16)
-        for i, coef in enumerate((12.0, 1.0, 180.0, DROP)):
-            ve.memset(T.rep[0:16, 128 * i:128 * i + 128], coef).then_inc(sem.s_rep, 1)
+        sy.dma_start(T.W[:, 0:WA], T.w1[:, 0:WA]).then_inc(sem.s_wa, 16)
+        se.dma_start(T.W[:, 512:1024], T.w2[:, :]).then_inc(sem.s_w, 16)
+        sy.dma_start(T.W[:, WA:512], T.w1[:, WA:512]).then_inc(sem.s_w, 16)
+        ve.memset(T.rep[0:16, :], 1.0).then_inc(sem.s_cf, 1)
+        for i, coef in enumerate((12.0, 180.0, DROP)):
+            ve.memset(T.repb[0:16, 128 * i:128 * i + 128], coef).then_inc(sem.s_cf, 1)
         ve.memset(T.S[:, 0:SLOTS], 0.0).then_inc(sem.s_set, 1)
-        ve.memset(T.R[:, SLOTS:SLOTS + 8], 0.0).then_inc(sem.s_set, 1)
-        g.wait_ge(sem.s_rep, 4)
-        g.affine_select(T.rep[0:16, :], T.rep[0:16, :], [[0, 32], [-1, 16]], Alu.is_equal, 0.0, 0, 1).then_inc(sem.s_g, 1)
+        g.wait_ge(sem.s_cf, 4)
+        g.affine_select(T.rep[0:16, :], T.rep[0:16, :], [[0, 8], [-1, 16]], Alu.is_equal, 0.0, 0, 1).then_inc(sem.s_g, 1)
+        g.affine_select(T.repb[0:16, :], T.repb[0:16, :], [[0, 24], [-1, 16]], Alu.is_equal, 0.0, 0, 1).then_inc(sem.s_g, 1)
         g.iota(T.q[:, :], [[16, 32]], SLOTS, 1, allow_small_or_imprecise_dtypes=True).then_inc(sem.s_g, 1)
         ve.wait_ge(sem.s_idx, 32)
-        ve.tensor_scalar(T.ai[0:16, :], T.idx[0:16, 0:32], 3, None, Alu.bitwise_and).then_inc(sem.s_d2, 1)
-        ve.tensor_copy(T.fl[0:16, 0:64], T.idx[0:16, 0:64]).then_inc(sem.s_f, 1)
-        ve.tensor_scalar(T.fl[0:16, 96:128], T.idx[0:16, 32:64], CAP, None, Alu.is_ge).then_inc(sem.s_f, 1)
-        ve.wait_ge(sem.s_d2, 1)
-        ve.tensor_copy(T.fl[0:16, 64:96], T.ai[0:16, :]).then_inc(sem.s_f, 1)
-        te.wait_ge(sem.s_g, 2)
-        te.wait_ge(sem.s_f, 3)
-        for i in range(4):
-            mm = te.matmul(T.zp[:, 0:32], T.rep[0:16, 128 * i:128 * i + 128], T.fl[0:16, 32 * i:32 * i + 32], i == 0, i == 3)
+        ve.tensor_scalar(T.ai[0:16, :], T.idx[0:16, 0:32], 3, None, Alu.bitwise_and).then_inc(sem.s_and, 1)
+        ve.tensor_copy(T.fl[0:16, :], T.idx[0:16, 32:64]).then_inc(sem.s_f, 1)
+        ve.tensor_copy(T.flb[0:16, 0:32], T.idx[0:16, 0:32]).then_inc(sem.s_f, 1)
+        ve.tensor_scalar(T.flb[0:16, 64:96], T.idx[0:16, 32:64], CAP, None, Alu.is_ge).then_inc(sem.s_f, 1)
+        ve.wait_ge(sem.s_and, 1)
+        ve.tensor_copy(T.flb[0:16, 32:64], T.ai[0:16, :]).then_inc(sem.s_f, 1)
+        te.wait_ge(sem.s_g, 3)
+        te.wait_ge(sem.s_f, 1)
+        te.matmul(T.zp[:, 0:32], T.rep[0:16, :], T.fl[0:16, :], True, False)
+        te.wait_ge(sem.s_f, 4)
+        for i in range(3):
+            mm = te.matmul(T.zp[:, 0:32], T.repb[0:16, 128 * i:128 * i + 128], T.flb[0:16, 32 * i:32 * i + 32], False, i == 2)
         mm.then_inc(sem.s_z, 1)
+        ve.wait_ge(sem.s_g, 3)
         ve.wait_ge(sem.s_z, 1)
-        ve.wait_ge(sem.s_g, 2)
         ve.tensor_tensor(T.zs[:, :], T.zp[:, 0:32], T.q[:, :], Alu.min).then_inc(sem.s_zs, 1)
         ve.wait_ge(sem.s_zs, 1)
         ve.tensor_copy(T.offs[:, :], T.zs[:, :]).then_inc(sem.s_off, 1)
         ve.wait_ge(sem.s_off, 1)
-        ve.wait_ge(sem.s_set, 2)
+        ve.wait_ge(sem.s_set, 1)
         ve.wait_ge(sem.s_x0, 16)
         ve.tensor_copy(T.S[:, 0:WIN].indirect(T.offs[:, 0:16]), T.xs[:, 0:256]).then_inc(sem.s_sc, 1)
         ve.wait_ge(sem.s_x1, 16)
         ve.wait_ge(sem.s_sc, 1)
         ve.tensor_copy(T.S[:, 0:WIN].indirect(T.offs[:, 16:32]), T.xs[:, 256:512]).then_inc(sem.s_sc, 1)
         ve.tensor_scalar(T.offg[:, :], T.zp[:, 0:32], float(SLOTS), None, Alu.min).then_inc(sem.s_og, 1)
+        ve.memset(T.R[:, SLOTS:SLOTS + 8], 0.0).then_inc(sem.s_og, 1)
+        g.wait_ge(sem.s_wa, 16)
+        send(other, T.W[:, 0:WA], T.W[:, 0:WA], sem.s_ws, bits(other))
         g.wait_ge(sem.s_sc, 2)
         g.remote_dma_fused([tr(host[ci][e], T.L[:, me, :, :], T.S[:, GRP * e:GRP * e + GRP], sem["p1_%d" % me],
-                               P1_ENG * e, P1_ENG) for e in range(NE) if host[ci][e] != core], local_sem=sem.lsem)
-        other = part[ci][me] if is_host else host[ci][me]
+                               bits(host[ci][e])[P1_ENG * e:P1_ENG * e + P1_ENG]) for e in range(NE) if host[ci][e] != core],
+                           local_sem=sem.lsem)
+        eng = bits(other)
+        half = len(eng) // 2
         g.wait_ge(sem.s_w, 32)
-        g.remote_dma_fused([tr(other, T.w1s[:, :], T.w1s[:, :], sem.s_ws, 0, W_ENG),
-                            tr(other, T.w2s[:, :], T.w2s[:, :], sem.s_ws, W_ENG, W_ENG)], local_sem=sem.lsem)
+        g.remote_dma_fused([tr(other, T.W[:, WA:WA + WR], T.W[:, WA:WA + WR], sem.s_ws, eng[0:half]),
+                            tr(other, T.W[:, WA + WR:WA + 2 * WR], T.W[:, WA + WR:WA + 2 * WR], sem.s_ws, eng[half:2 * half])],
+                           local_sem=sem.lsem)
 
     n_m = n_ml = 0
     if is_host:
@@ -166,23 +179,25 @@ def rank_program(g, core, T, topo):
         g.wait_ge(sem.s_m, n_m)
         for c in P["cross"][ci] + P["plane"][ci]:
             dst = host[c][ex] if c in P["cross"][ci] else part[c][ex]
-            send(dst, T.V[:, GRP * ci:GRP * ci + GRP], T.M[:, c, :, :], sem["p2_%d" % ci], OFF_ENG)
+            send(dst, T.V[:, GRP * ci:GRP * ci + GRP], T.M[:, c, :, :], sem["p2_%d" % ci], bits(dst)[0:OFF_ENG])
 
     if is_host:
         groups = [(ci, [(sem.s_m, n_m), (sem.s_ml, n_ml)])] + [(a, [(sem["p2_%d" % a], OFF_ENG)]) for a in P["take"][ci]]
     else:
         groups = [(a, [(sem["p2_%d" % a], OFF_ENG)]) for a in P["plane"][ci]]
     if is_rank:
+        te.wait_ge(sem.s_wa, 16)
         te.wait_ge(sem.s_w, 32)
     else:
-        te.wait_ge(sem.s_ws, 2 * W_ENG)
+        n_eng = len(bits(core, rc[ci][ex]))
+        te.wait_ge(sem.s_ws, n_eng + 2 * (n_eng // 2))
     hp = [T.hp0, T.hp1, T.hp2, T.hp3]
     op = [T.op0, T.op1]
     for n, (c, waits) in enumerate(groups):
         for s_, v_ in waits:
             te.wait_ge(s_, v_)
         for f in range(FF):
-            te.matmul(hp[f][:, 0:GRP], T.w1s[:, 128 * f:128 * f + 128], T.V[:, GRP * c:GRP * c + GRP], True, True).then_inc(sem.s_l1, 1)
+            te.matmul(hp[f][:, 0:GRP], T.W[:, 128 * f:128 * f + 128], T.V[:, GRP * c:GRP * c + GRP], True, True).then_inc(sem.s_l1, 1)
         for f in range(FF):
             hb = T.h[:, ((n % 2) * FF + f) * GRP:((n % 2) * FF + f) * GRP + GRP]
             eng = se if f % 2 == 0 else ve
@@ -198,7 +213,7 @@ def rank_program(g, core, T, topo):
         for f in range(FF):
             hb = T.h[:, ((n % 2) * FF + f) * GRP:((n % 2) * FF + f) * GRP + GRP]
             te.wait_ge(sem.s_ra if f % 2 == 0 else sem.s_rv, 2 * n + f // 2 + 1)
-            te.matmul(op[n % 2][:, 0:GRP], T.w2s[:, 128 * f:128 * f + 128], hb, f == 0, f == FF - 1).then_inc(sem.s_l2, 1)
+            te.matmul(op[n % 2][:, 0:GRP], T.W[:, 512 + 128 * f:512 + 128 * f + 128], hb, f == 0, f == FF - 1).then_inc(sem.s_l2, 1)
         ve.wait_ge(sem.s_l2, FF * n + FF)
         ve.tensor_copy(T.OB[:, GRP * c:GRP * c + GRP], op[n % 2][:, 0:GRP]).then_inc(sem.s_o, 1)
 
@@ -209,7 +224,8 @@ def rank_program(g, core, T, topo):
 
     def forward(buf, x):
         g.remote_dma_fused([tr(rc[ci][s], T.R[:, rcol(ex, x):rcol(ex, x) + CAP], buf[:, GRP * x + CAP * s:GRP * x + CAP * s + CAP],
-                               sem.r2, FWD_ENG * s, FWD_ENG) for s in range(NE) if rc[ci][s] != core], local_sem=sem.lsem)
+                               sem.r2, bits(rc[ci][s])[FWD_ENG * s:FWD_ENG * s + FWD_ENG]) for s in range(NE) if rc[ci][s] != core],
+                           local_sem=sem.lsem)
 
     for n, (c, _) in enumerate(groups):
         g.wait_ge(sem.s_o, n + 1)
@@ -219,12 +235,10 @@ def rank_program(g, core, T, topo):
                 ve.wait_ge(sem.s_o, len(groups))
                 ve.tensor_copy(T.R[:, rcol(ex, ci):rcol(ex, ci) + CAP], T.OB[:, GRP * ci + CAP * me:GRP * ci + CAP * me + CAP]).then_inc(sem.s_self, 1)
                 n_self += 1
-        elif RET_DIRECT:
-            g.remote_dma_fused([tr(rc[c][s], T.R[:, rcol(ex, ci):rcol(ex, ci) + CAP], T.OB[:, GRP * c + CAP * s:GRP * c + CAP * s + CAP],
-                                   sem.r2, DIR_ENG * s, DIR_ENG) for s in range(NE)], local_sem=sem.lsem)
         else:
-            send(host[c][ex], T.RL[:, GRP * ci:GRP * ci + GRP], T.OB[:, GRP * c:GRP * c + GRP], sem["r1_%d" % ci], OFF_ENG)
-    if is_host and not RET_DIRECT:
+            send(host[c][ex], T.RL[:, GRP * ci:GRP * ci + GRP], T.OB[:, GRP * c:GRP * c + GRP], sem["r1_%d" % ci],
+                 bits(host[c][ex])[0:OFF_ENG])
+    if is_host:
         for x in P["back"][ci]:
             g.wait_ge(sem["r1_%d" % x], OFF_ENG)
             forward(T.RL, x)
@@ -234,19 +248,12 @@ def rank_program(g, core, T, topo):
                 n_self += 1
 
     if is_rank:
-        total = 0
-        for e in range(NE):
-            for x in range(4):
-                if x == ci or not RET_DIRECT:
-                    total += 0 if host[ci][e] == core else FWD_ENG
-                else:
-                    total += DIR_ENG
+        total = sum(4 * FWD_ENG for e in range(NE) if host[ci][e] != core)
         for eng in (ve, se):
             eng.wait_ge(sem.r2, total)
             if n_self:
                 eng.wait_ge(sem.s_self, n_self)
-            eng.wait_ge(sem.s_og, 1)
-            eng.wait_ge(sem.s_set, 2)
+            eng.wait_ge(sem.s_og, 2)
         ve.tensor_copy(T.ys[:, 0:256], T.R[:, 0:SLOTS + 8].indirect(T.offg[:, 0:16])).then_inc(sem.s_gv, 1)
         se.activation(T.ys[:, 256:512], T.R[:, 0:SLOTS + 8].indirect(T.offg[:, 16:32]), Act.Copy).then_inc(sem.s_ga, 1)
         sy.wait_ge(sem.s_gv, 1)

@@ -7,9 +7,11 @@ GRP = NE * CAP
 SLOTS = 16 * CAP
 WIN = SLOTS + 128 + 16 * 31
 DROP = 8192.0
-P1_ENG, FWD_ENG, OFF_ENG = 4, 4, 8
+P1_ENG, OFF_ENG = 4, 8
 WA = 128
 WR = (2 * FF * 128 - WA) // 2
+WHOLE = [(0, NE)]
+HALVES = [(0, NE // 2), (NE // 2, NE // 2)]
 
 SCRATCH = {
     "idx": ("sbuf", [128, 64], "int32"),
@@ -67,7 +69,10 @@ def plan(T, topo):
              for a in range(n)]
     take = [sorted(cross[x], key=lambda a, x=x: (cross[a].index(x), (x - a) % n)) for x in range(n)]
     back = [sorted(cross[a], key=lambda x, a=a: (take[x].index(a), (x - a) % n)) + plane[a] for a in range(n)]
-    return dict(chips=chips, rc=rc, host=host, part=part, plane=plane, cross=cross, take=take, back=back)
+
+    def cut(x, a):
+        return HALVES if a in (take[x][-1:] + plane[x][-1:]) else WHOLE
+    return dict(chips=chips, rc=rc, host=host, part=part, plane=plane, cross=cross, take=take, back=back, cut=cut)
 
 
 def rank_program(g, core, T, topo):
@@ -75,7 +80,7 @@ def rank_program(g, core, T, topo):
     if topo.chip(core) not in P["chips"]:
         return
     ci = P["chips"].index(topo.chip(core))
-    rc, host, part = P["rc"], P["host"], P["part"]
+    rc, host, part, cut = P["rc"], P["host"], P["part"], P["cut"]
     is_rank, is_host, is_part = core in rc[ci], core in host[ci], core in part[ci]
     if not (is_rank or is_host or is_part):
         return
@@ -181,10 +186,12 @@ def rank_program(g, core, T, topo):
             dst = host[c][ex] if c in P["cross"][ci] else part[c][ex]
             send(dst, T.V[:, GRP * ci:GRP * ci + GRP], T.M[:, c, :, :], sem["p2_%d" % ci], bits(dst)[0:OFF_ENG])
 
+    pieces = []
     if is_host:
-        groups = [(ci, [(sem.s_m, n_m), (sem.s_ml, n_ml)])] + [(a, [(sem["p2_%d" % a], OFF_ENG)]) for a in P["take"][ci]]
-    else:
-        groups = [(a, [(sem["p2_%d" % a], OFF_ENG)]) for a in P["plane"][ci]]
+        pieces.append((ci, 0, NE, [(sem.s_m, n_m), (sem.s_ml, n_ml)]))
+    for a in (P["take"][ci] if is_host else P["plane"][ci]):
+        for s0, ns in cut(ci, a):
+            pieces.append((a, s0, ns, [(sem["p2_%d" % a], OFF_ENG)]))
     if is_rank:
         te.wait_ge(sem.s_wa, 16)
         te.wait_ge(sem.s_w, 32)
@@ -193,66 +200,80 @@ def rank_program(g, core, T, topo):
         te.wait_ge(sem.s_ws, n_eng + 2 * (n_eng // 2))
     hp = [T.hp0, T.hp1, T.hp2, T.hp3]
     op = [T.op0, T.op1]
-    for n, (c, waits) in enumerate(groups):
+    for n, (c, s0, ns, waits) in enumerate(pieces):
+        lo, w = GRP * c + CAP * s0, CAP * ns
         for s_, v_ in waits:
             te.wait_ge(s_, v_)
         for f in range(FF):
-            te.matmul(hp[f][:, 0:GRP], T.W[:, 128 * f:128 * f + 128], T.V[:, GRP * c:GRP * c + GRP], True, True).then_inc(sem.s_l1, 1)
+            te.matmul(hp[f][:, 0:w], T.W[:, 128 * f:128 * f + 128], T.V[:, lo:lo + w], True, True).then_inc(sem.s_l1, 1)
         for f in range(FF):
-            hb = T.h[:, ((n % 2) * FF + f) * GRP:((n % 2) * FF + f) * GRP + GRP]
+            hb = T.h[:, ((n % 2) * FF + f) * GRP:((n % 2) * FF + f) * GRP + w]
             eng = se if f % 2 == 0 else ve
             eng.wait_ge(sem.s_l1, FF * n + f + 1)
             if n >= 2:
                 eng.wait_ge(sem.s_l2, FF * (n - 2) + f + 1)
             if f % 2 == 0:
-                se.activation(hb, hp[f][:, 0:GRP], Act.Relu).then_inc(sem.s_ra, 1)
+                se.activation(hb, hp[f][:, 0:w], Act.Relu).then_inc(sem.s_ra, 1)
             else:
-                ve.tensor_scalar(hb, hp[f][:, 0:GRP], 0.0, None, Alu.max).then_inc(sem.s_rv, 1)
+                ve.tensor_scalar(hb, hp[f][:, 0:w], 0.0, None, Alu.max).then_inc(sem.s_rv, 1)
         if n >= 2:
             te.wait_ge(sem.s_o, n - 1)
         for f in range(FF):
-            hb = T.h[:, ((n % 2) * FF + f) * GRP:((n % 2) * FF + f) * GRP + GRP]
+            hb = T.h[:, ((n % 2) * FF + f) * GRP:((n % 2) * FF + f) * GRP + w]
             te.wait_ge(sem.s_ra if f % 2 == 0 else sem.s_rv, 2 * n + f // 2 + 1)
-            te.matmul(op[n % 2][:, 0:GRP], T.W[:, 512 + 128 * f:512 + 128 * f + 128], hb, f == 0, f == FF - 1).then_inc(sem.s_l2, 1)
+            te.matmul(op[n % 2][:, 0:w], T.W[:, 512 + 128 * f:512 + 128 * f + 128], hb, f == 0, f == FF - 1).then_inc(sem.s_l2, 1)
         ve.wait_ge(sem.s_l2, FF * n + FF)
-        ve.tensor_copy(T.OB[:, GRP * c:GRP * c + GRP], op[n % 2][:, 0:GRP]).then_inc(sem.s_o, 1)
+        ve.tensor_copy(T.OB[:, lo:lo + w], op[n % 2][:, 0:w]).then_inc(sem.s_o, 1)
 
     def rcol(e, x):
         return GRP * e + CAP * x
 
-    n_self = 0
+    n_self = [0]
 
-    def forward(buf, x):
-        g.remote_dma_fused([tr(rc[ci][s], T.R[:, rcol(ex, x):rcol(ex, x) + CAP], buf[:, GRP * x + CAP * s:GRP * x + CAP * s + CAP],
-                               sem.r2, bits(rc[ci][s])[FWD_ENG * s:FWD_ENG * s + FWD_ENG]) for s in range(NE) if rc[ci][s] != core],
-                           local_sem=sem.lsem)
+    def deliver(buf, x, c, s0, ns):
+        trs = []
+        for s in range(s0, s0 + ns):
+            src = buf[:, GRP * (x if c == ci else c) + CAP * s:GRP * (x if c == ci else c) + CAP * s + CAP]
+            if rc[c][s] == core:
+                ve.tensor_copy(T.R[:, rcol(ex, x):rcol(ex, x) + CAP], src).then_inc(sem.s_self, 1)
+                n_self[0] += 1
+            else:
+                eng = bits(rc[c][s])
+                wd = len(eng) // ns
+                trs.append(tr(rc[c][s], T.R[:, rcol(ex, x):rcol(ex, x) + CAP], src, sem.r2, eng[wd * (s - s0):wd * (s - s0) + wd]))
+        g.remote_dma_fused(trs, local_sem=sem.lsem)
 
-    for n, (c, _) in enumerate(groups):
+    for n, (c, s0, ns, _) in enumerate(pieces):
         g.wait_ge(sem.s_o, n + 1)
         if c == ci:
-            forward(T.OB, ci)
-            if is_rank:
-                ve.wait_ge(sem.s_o, len(groups))
-                ve.tensor_copy(T.R[:, rcol(ex, ci):rcol(ex, ci) + CAP], T.OB[:, GRP * ci + CAP * me:GRP * ci + CAP * me + CAP]).then_inc(sem.s_self, 1)
-                n_self += 1
+            ve.wait_ge(sem.s_o, len(pieces))
+            deliver(T.OB, ci, ci, s0, ns)
+        elif len(cut(ci, c)) > 1:
+            deliver(T.OB, ci, c, s0, ns)
         else:
             send(host[c][ex], T.RL[:, GRP * ci:GRP * ci + GRP], T.OB[:, GRP * c:GRP * c + GRP], sem["r1_%d" % ci],
                  bits(host[c][ex])[0:OFF_ENG])
     if is_host:
         for x in P["back"][ci]:
-            g.wait_ge(sem["r1_%d" % x], OFF_ENG)
-            forward(T.RL, x)
-            if is_rank:
-                ve.wait_ge(sem["r1_%d" % x], OFF_ENG)
-                ve.tensor_copy(T.R[:, rcol(ex, x):rcol(ex, x) + CAP], T.RL[:, GRP * x + CAP * me:GRP * x + CAP * me + CAP]).then_inc(sem.s_self, 1)
-                n_self += 1
+            if len(cut(x, ci)) == 1:
+                g.wait_ge(sem["r1_%d" % x], OFF_ENG)
+                if is_rank:
+                    ve.wait_ge(sem["r1_%d" % x], OFF_ENG)
+                deliver(T.RL, x, ci, 0, NE)
 
     if is_rank:
-        total = sum(4 * FWD_ENG for e in range(NE) if host[ci][e] != core)
+        total = 0
+        for e in range(NE):
+            for x in range(4):
+                if x == ci or len(cut(x, ci)) == 1:
+                    total += 0 if host[ci][e] == core else len(bits(core, host[ci][e])) // NE
+                else:
+                    frm = host[x][e] if ci in P["cross"][x] else part[x][e]
+                    total += sum(len(bits(core, frm)) // ns for s0, ns in cut(x, ci) if s0 <= me < s0 + ns)
         for eng in (ve, se):
             eng.wait_ge(sem.r2, total)
-            if n_self:
-                eng.wait_ge(sem.s_self, n_self)
+            if n_self[0]:
+                eng.wait_ge(sem.s_self, n_self[0])
             eng.wait_ge(sem.s_og, 2)
         ve.tensor_copy(T.ys[:, 0:256], T.R[:, 0:SLOTS + 8].indirect(T.offg[:, 0:16])).then_inc(sem.s_gv, 1)
         se.activation(T.ys[:, 256:512], T.R[:, 0:SLOTS + 8].indirect(T.offg[:, 16:32]), Act.Copy).then_inc(sem.s_ga, 1)

@@ -14,12 +14,10 @@ WHOLE = [(0, NE)]
 HALVES = [(0, NE // 2), (NE // 2, NE // 2)]
 
 SCRATCH = {
-    "idx": ("sbuf", [128, 64], "int32"),
-    "ai": ("sbuf", [128, 32], "int32"),
-    "fl": ("sbuf", [128, 32], "float32"),
-    "flb": ("sbuf", [128, 96], "bfloat16"),
-    "rep": ("sbuf", [128, 128], "float32"),
-    "repb": ("sbuf", [128, 384], "bfloat16"),
+    "idx": ("sbuf", [128, 96], "int32"),
+    "flb": ("sbuf", [128, 128], "bfloat16"),
+    "dv": ("sbuf", [128, 128], "bfloat16"),
+    "repb": ("sbuf", [128, 512], "bfloat16"),
     "q": ("sbuf", [128, 32], "float32"),
     "zs": ("sbuf", [128, 32], "float32"),
     "offs": ("sbuf", [128, 32], "uint16"),
@@ -43,7 +41,7 @@ SCRATCH = {
     "op1": ("psum", [128, 512], "float32"),
     "zp": ("psum", [128, 512], "float32"),
 }
-SEMAPHORES = ["s_idx", "s_x0", "s_x1", "s_wa", "s_w", "s_ws", "s_cf", "s_and", "s_set", "s_g", "s_f", "s_z",
+SEMAPHORES = ["s_idx", "s_x0", "s_wa", "s_w", "s_ws", "s_cf", "s_and", "s_set", "s_g", "s_q", "s_f", "s_z",
               "s_zs", "s_off", "s_sc", "s_og", "s_m", "s_ml", "s_l1", "s_l2", "s_ra", "s_rv", "s_o", "s_self", "s_gv",
               "s_ga", "s_y", "lsem", "r2"] + ["p1_%d" % i for i in range(4)] + ["p2_%d" % i for i in range(4)] + \
              ["r1_%d" % i for i in range(4)]
@@ -94,6 +92,10 @@ def rank_program(g, core, T, topo):
         m = topo.mask(src, dst)
         return [b for b in range(m.bit_length()) if (m >> b) & 1]
 
+    def home(dst, src=core):
+        far = bits(next(c for c in T.cores if topo.chip(c) != topo.chip(src)), src)
+        return [b for b in bits(dst, src) if b not in far] or bits(dst, src)
+
     def tr(dst, out, in_, rsem, eng):
         rid, pid, _ = topo.addr(dst)
         sent[0] += len(eng)
@@ -109,34 +111,29 @@ def rank_program(g, core, T, topo):
         other = part[ci][me] if is_host else host[ci][me]
         sy.dma_start(T.idx[0:16, 0:32], T.ex[:, :]).then_inc(sem.s_idx, 16)
         se.dma_start(T.idx[0:16, 32:64], T.pos[:, :]).then_inc(sem.s_idx, 16)
-        sy.dma_start(T.xs[:, 0:256], T.x[:, 0:256]).then_inc(sem.s_x0, 16)
-        se.dma_start(T.xs[:, 256:512], T.x[:, 256:512]).then_inc(sem.s_x1, 16)
-        sy.dma_start(T.W[:, 0:WA], T.w1[:, 0:WA]).then_inc(sem.s_wa, 16)
+        sy.dma_start(T.xs[:, :], T.x[:, :]).then_inc(sem.s_x0, 16)
+        se.dma_start(T.W[:, 0:WA], T.w1[:, 0:WA]).then_inc(sem.s_wa, 16)
         se.dma_start(T.W[:, 512:1024], T.w2[:, :]).then_inc(sem.s_w, 16)
         sy.dma_start(T.W[:, WA:512], T.w1[:, WA:512]).then_inc(sem.s_w, 16)
-        ve.memset(T.rep[0:16, :], 1.0).then_inc(sem.s_cf, 1)
-        for i, coef in enumerate((12.0, 180.0, DROP)):
-            ve.memset(T.repb[0:16, 128 * i:128 * i + 128], coef).then_inc(sem.s_cf, 1)
+        g.iota(T.dv[0:16, :], [[0, 8], [1, 16]], 0, -1, allow_small_or_imprecise_dtypes=True).then_inc(sem.s_g, 1)
+        g.iota(T.q[:, :], [[16, 32]], SLOTS, 1, allow_small_or_imprecise_dtypes=True).then_inc(sem.s_q, 1)
         ve.memset(T.S[:, 0:SLOTS], 0.0).then_inc(sem.s_set, 1)
-        g.wait_ge(sem.s_cf, 4)
-        g.affine_select(T.rep[0:16, :], T.rep[0:16, :], [[0, 8], [-1, 16]], Alu.is_equal, 0.0, 0, 1).then_inc(sem.s_g, 1)
-        g.affine_select(T.repb[0:16, :], T.repb[0:16, :], [[0, 24], [-1, 16]], Alu.is_equal, 0.0, 0, 1).then_inc(sem.s_g, 1)
-        g.iota(T.q[:, :], [[16, 32]], SLOTS, 1, allow_small_or_imprecise_dtypes=True).then_inc(sem.s_g, 1)
+        ve.wait_ge(sem.s_g, 1)
+        for i, coef in enumerate((DROP, 12.0, 1.0, 180.0)):
+            ve.tensor_scalar(T.repb[0:16, 128 * i:128 * i + 128], T.dv[0:16, :], 0.0, coef, Alu.is_equal, Alu.mult).then_inc(sem.s_cf, 1)
         ve.wait_ge(sem.s_idx, 32)
-        ve.tensor_scalar(T.ai[0:16, :], T.idx[0:16, 0:32], 3, None, Alu.bitwise_and).then_inc(sem.s_and, 1)
-        ve.tensor_copy(T.fl[0:16, :], T.idx[0:16, 32:64]).then_inc(sem.s_f, 1)
-        ve.tensor_copy(T.flb[0:16, 0:32], T.idx[0:16, 0:32]).then_inc(sem.s_f, 1)
-        ve.tensor_scalar(T.flb[0:16, 64:96], T.idx[0:16, 32:64], CAP, None, Alu.is_ge).then_inc(sem.s_f, 1)
+        ve.tensor_scalar(T.idx[0:16, 64:96], T.idx[0:16, 0:32], 3, None, Alu.bitwise_and).then_inc(sem.s_and, 1)
+        ve.tensor_scalar(T.flb[0:16, 0:32], T.idx[0:16, 32:64], CAP, None, Alu.is_ge).then_inc(sem.s_f, 1)
         ve.wait_ge(sem.s_and, 1)
-        ve.tensor_copy(T.flb[0:16, 32:64], T.ai[0:16, :]).then_inc(sem.s_f, 1)
-        te.wait_ge(sem.s_g, 3)
+        ve.tensor_scalar(T.flb[0:16, 32:128], T.idx[0:16, 0:96], CAP, None, Alu.min).then_inc(sem.s_f, 1)
+        te.wait_ge(sem.s_cf, 4)
         te.wait_ge(sem.s_f, 1)
-        te.matmul(T.zp[:, 0:32], T.rep[0:16, :], T.fl[0:16, :], True, False)
-        te.wait_ge(sem.s_f, 4)
-        for i in range(3):
-            mm = te.matmul(T.zp[:, 0:32], T.repb[0:16, 128 * i:128 * i + 128], T.flb[0:16, 32 * i:32 * i + 32], False, i == 2)
+        te.matmul(T.zp[:, 0:32], T.repb[0:16, 0:128], T.flb[0:16, 0:32], True, False)
+        te.wait_ge(sem.s_f, 2)
+        for i in range(1, 4):
+            mm = te.matmul(T.zp[:, 0:32], T.repb[0:16, 128 * i:128 * i + 128], T.flb[0:16, 32 * i:32 * i + 32], False, i == 3)
         mm.then_inc(sem.s_z, 1)
-        ve.wait_ge(sem.s_g, 3)
+        ve.wait_ge(sem.s_q, 1)
         ve.wait_ge(sem.s_z, 1)
         ve.tensor_tensor(T.zs[:, :], T.zp[:, 0:32], T.q[:, :], Alu.min).then_inc(sem.s_zs, 1)
         ve.wait_ge(sem.s_zs, 1)
@@ -144,29 +141,29 @@ def rank_program(g, core, T, topo):
         ve.wait_ge(sem.s_off, 1)
         ve.wait_ge(sem.s_set, 1)
         ve.wait_ge(sem.s_x0, 16)
-        ve.tensor_copy(T.S[:, 0:WIN].indirect(T.offs[:, 0:16]), T.xs[:, 0:256]).then_inc(sem.s_sc, 1)
-        ve.wait_ge(sem.s_x1, 16)
-        ve.wait_ge(sem.s_sc, 1)
-        ve.tensor_copy(T.S[:, 0:WIN].indirect(T.offs[:, 16:32]), T.xs[:, 256:512]).then_inc(sem.s_sc, 1)
+        ve.tensor_copy(T.S[:, 0:WIN].indirect(T.offs[:, 0:32]), T.xs[:, :]).then_inc(sem.s_sc, 1)
         ve.tensor_scalar(T.offg[:, :], T.zp[:, 0:32], float(SLOTS), None, Alu.min).then_inc(sem.s_og, 1)
         ve.memset(T.R[:, SLOTS:SLOTS + 8], 0.0).then_inc(sem.s_og, 1)
         g.wait_ge(sem.s_wa, 16)
         send(other, T.W[:, 0:WA], T.W[:, 0:WA], sem.s_ws, bits(other))
-        g.wait_ge(sem.s_sc, 2)
+        g.wait_ge(sem.s_sc, 1)
         g.remote_dma_fused([tr(host[ci][e], T.L[:, me, :, :], T.S[:, GRP * e:GRP * e + GRP], sem["p1_%d" % me],
                                bits(host[ci][e])[P1_ENG * e:P1_ENG * e + P1_ENG]) for e in range(NE) if host[ci][e] != core],
                            local_sem=sem.lsem)
         eng = bits(other)
         half = len(eng) // 2
         g.wait_ge(sem.s_w, 32)
-        g.remote_dma_fused([tr(other, T.W[:, WA:WA + WR], T.W[:, WA:WA + WR], sem.s_ws, eng[0:half]),
-                            tr(other, T.W[:, WA + WR:WA + 2 * WR], T.W[:, WA + WR:WA + 2 * WR], sem.s_ws, eng[half:2 * half])],
-                           local_sem=sem.lsem)
+        if is_host:
+            send(other, T.W[:, WA:WA + 2 * WR], T.W[:, WA:WA + 2 * WR], sem.s_ws, home(other))
+        else:
+            g.remote_dma_fused([tr(other, T.W[:, WA:WA + WR], T.W[:, WA:WA + WR], sem.s_ws, eng[0:half]),
+                                tr(other, T.W[:, WA + WR:WA + 2 * WR], T.W[:, WA + WR:WA + 2 * WR], sem.s_ws, eng[half:2 * half])],
+                               local_sem=sem.lsem)
 
     n_m = n_ml = 0
     if is_host:
         if is_rank:
-            ve.wait_ge(sem.s_sc, 2)
+            ve.wait_ge(sem.s_sc, 1)
             for c in range(4):
                 src = T.S[:, GRP * ex + CAP * c:GRP * ex + CAP * c + CAP]
                 out = T.V[:, GRP * ci + CAP * me:GRP * ci + CAP * me + CAP] if c == ci else T.M[:, c, me, :]
@@ -197,7 +194,7 @@ def rank_program(g, core, T, topo):
         te.wait_ge(sem.s_w, 32)
     else:
         n_eng = len(bits(core, rc[ci][ex]))
-        te.wait_ge(sem.s_ws, n_eng + 2 * (n_eng // 2))
+        te.wait_ge(sem.s_ws, n_eng + (2 * (n_eng // 2) if is_host else len(home(core, rc[ci][ex]))))
     hp = [T.hp0, T.hp1, T.hp2, T.hp3]
     op = [T.op0, T.op1]
     for n, (c, s0, ns, waits) in enumerate(pieces):
@@ -230,7 +227,7 @@ def rank_program(g, core, T, topo):
 
     n_self = [0]
 
-    def deliver(buf, x, c, s0, ns):
+    def deliver(buf, x, c, s0, ns, pick=bits):
         trs = []
         for s in range(s0, s0 + ns):
             src = buf[:, GRP * (x if c == ci else c) + CAP * s:GRP * (x if c == ci else c) + CAP * s + CAP]
@@ -238,7 +235,7 @@ def rank_program(g, core, T, topo):
                 ve.tensor_copy(T.R[:, rcol(ex, x):rcol(ex, x) + CAP], src).then_inc(sem.s_self, 1)
                 n_self[0] += 1
             else:
-                eng = bits(rc[c][s])
+                eng = pick(rc[c][s])
                 wd = len(eng) // ns
                 trs.append(tr(rc[c][s], T.R[:, rcol(ex, x):rcol(ex, x) + CAP], src, sem.r2, eng[wd * (s - s0):wd * (s - s0) + wd]))
         g.remote_dma_fused(trs, local_sem=sem.lsem)
@@ -247,7 +244,7 @@ def rank_program(g, core, T, topo):
         g.wait_ge(sem.s_o, n + 1)
         if c == ci:
             ve.wait_ge(sem.s_o, len(pieces))
-            deliver(T.OB, ci, ci, s0, ns)
+            deliver(T.OB, ci, ci, s0, ns, home)
         elif len(cut(ci, c)) > 1:
             deliver(T.OB, ci, c, s0, ns)
         else:
@@ -266,7 +263,7 @@ def rank_program(g, core, T, topo):
         for e in range(NE):
             for x in range(4):
                 if x == ci or len(cut(x, ci)) == 1:
-                    total += 0 if host[ci][e] == core else len(bits(core, host[ci][e])) // NE
+                    total += 0 if host[ci][e] == core else len((home if x == ci else bits)(core, host[ci][e])) // NE
                 else:
                     frm = host[x][e] if ci in P["cross"][x] else part[x][e]
                     total += sum(len(bits(core, frm)) // ns for s0, ns in cut(x, ci) if s0 <= me < s0 + ns)
@@ -278,9 +275,8 @@ def rank_program(g, core, T, topo):
         ve.tensor_copy(T.ys[:, 0:256], T.R[:, 0:SLOTS + 8].indirect(T.offg[:, 0:16])).then_inc(sem.s_gv, 1)
         se.activation(T.ys[:, 256:512], T.R[:, 0:SLOTS + 8].indirect(T.offg[:, 16:32]), Act.Copy).then_inc(sem.s_ga, 1)
         sy.wait_ge(sem.s_gv, 1)
-        sy.dma_start(T.y[:, 0:256], T.ys[:, 0:256]).then_inc(sem.s_y, 16)
-        se.wait_ge(sem.s_ga, 1)
-        se.dma_start(T.y[:, 256:512], T.ys[:, 256:512]).then_inc(sem.s_y, 16)
-        sy.wait_ge(sem.s_y, 32)
+        sy.wait_ge(sem.s_ga, 1)
+        sy.dma_start(T.y[:, :], T.ys[:, :]).then_inc(sem.s_y, 16)
+        sy.wait_ge(sem.s_y, 16)
     if sent[0]:
         g.wait_ge(sem.lsem, sent[0])

from concourse.bass import DstId, RemoteDMATransfer
from concourse.mybir import AluOpType, ActivationFunctionType

TOK, CAP, FF = 512, 48, 4
NE = 4
GRP = NE * CAP
SLOTS = 16 * CAP
WIN = SLOTS + 128 + 16 * 31
DROP = 8192.0
P1_ENG, OFF_ENG = 4, 8
WA = 128
WR = (2 * FF * 128 - WA) // 2
WHOLE = [(0, NE)]
HALVES = [(0, NE // 2), (NE // 2, NE // 2)]

SCRATCH = {
    "idx": ("sbuf", [128, 96], "int32"),
    "flb": ("sbuf", [128, 128], "bfloat16"),
    "dv": ("sbuf", [128, 128], "bfloat16"),
    "repb": ("sbuf", [128, 512], "bfloat16"),
    "q": ("sbuf", [128, 32], "float32"),
    "zs": ("sbuf", [128, 32], "float32"),
    "offs": ("sbuf", [128, 32], "uint16"),
    "offg": ("sbuf", [128, 32], "uint16"),
    "xs": ("sbuf", [128, TOK], "bfloat16"),
    "ys": ("sbuf", [128, TOK], "bfloat16"),
    "S": ("sbuf", [128, WIN], "bfloat16"),
    "R": ("sbuf", [128, SLOTS + 8], "bfloat16"),
    "W": ("sbuf", [128, 2 * FF * 128], "bfloat16"),
    "L": ("sbuf", [128, NE, 4, CAP], "bfloat16"),
    "M": ("sbuf", [128, 4, NE, CAP], "bfloat16"),
    "V": ("sbuf", [128, 4 * GRP], "bfloat16"),
    "h": ("sbuf", [128, 2 * FF * GRP], "bfloat16"),
    "OB": ("sbuf", [128, 4 * GRP], "bfloat16"),
    "RL": ("sbuf", [128, 4 * GRP], "bfloat16"),
    "hp0": ("psum", [128, 512], "float32"),
    "hp1": ("psum", [128, 512], "float32"),
    "hp2": ("psum", [128, 512], "float32"),
    "hp3": ("psum", [128, 512], "float32"),
    "op0": ("psum", [128, 512], "float32"),
    "op1": ("psum", [128, 512], "float32"),
    "zp": ("psum", [128, 512], "float32"),
}
SEMAPHORES = ["s_idx", "s_x0", "s_wa", "s_w", "s_ws", "s_cf", "s_and", "s_set", "s_g", "s_q", "s_f", "s_z",
              "s_zs", "s_off", "s_sc", "s_og", "s_m", "s_ml", "s_l1", "s_l2", "s_ra", "s_rv", "s_o", "s_self", "s_gv",
              "s_ga", "s_y", "lsem", "r2"] + ["p1_%d" % i for i in range(4)] + ["p2_%d" % i for i in range(4)] + \
             ["r1_%d" % i for i in range(4)]


def plan(T, topo):
    cores = list(T.cores)
    chips = sorted(set(topo.chip(c) for c in cores))
    n = len(chips)
    rc = [[c for c in cores if topo.chip(c) == ch] for ch in chips]
    everyone = range(topo.CORES_PER_CHIP * topo.CHIPS)
    host, part = [], []
    for i, ch in enumerate(chips):
        far = [c for c in cores if topo.chip(c) != ch and not topo.same_plane(ch, topo.chip(c))]
        mine = [c for c in everyone if topo.chip(c) == ch]
        port = [c for c in mine if all(topo.may_write(c, d) for d in far)]
        free_port = [c for c in port if c not in rc[i]]
        free_rest = [c for c in mine if c not in port and c not in rc[i]]
        host.append([c if c in port else free_port.pop(0) for c in rc[i]])
        part.append([c if c not in port else free_rest.pop(0) for c in rc[i]])
    plane = [[b for b in range(n) if b != a and topo.same_plane(chips[a], chips[b])] for a in range(n)]
    cross = [sorted([b for b in range(n) if b != a and b not in plane[a]], key=lambda b, a=a: (b - a) % n)
             for a in range(n)]
    take = [sorted(cross[x], key=lambda a, x=x: (cross[a].index(x), (x - a) % n)) for x in range(n)]
    back = [sorted(cross[a], key=lambda x, a=a: (take[x].index(a), (x - a) % n)) + plane[a] for a in range(n)]

    def cut(x, a):
        return HALVES if a in (take[x][-1:] + plane[x][-1:]) else WHOLE
    return dict(chips=chips, rc=rc, host=host, part=part, plane=plane, cross=cross, take=take, back=back, cut=cut)


def rank_program(g, core, T, topo):
    P = plan(T, topo)
    if topo.chip(core) not in P["chips"]:
        return
    ci = P["chips"].index(topo.chip(core))
    rc, host, part, cut = P["rc"], P["host"], P["part"], P["cut"]
    is_rank, is_host, is_part = core in rc[ci], core in host[ci], core in part[ci]
    if not (is_rank or is_host or is_part):
        return
    sem, ve, se, te, sy = T.sem, g.vector, g.scalar, g.tensor, g.sync
    Alu, Act = AluOpType, ActivationFunctionType
    me = rc[ci].index(core) if is_rank else None
    ex = host[ci].index(core) if is_host else part[ci].index(core)
    sent = [0]

    def bits(dst, src=core):
        m = topo.mask(src, dst)
        return [b for b in range(m.bit_length()) if (m >> b) & 1]

    def home(dst, src=core):
        far = bits(next(c for c in T.cores if topo.chip(c) != topo.chip(src)), src)
        return [b for b in bits(dst, src) if b not in far] or bits(dst, src)

    def tr(dst, out, in_, rsem, eng):
        rid, pid, _ = topo.addr(dst)
        sent[0] += len(eng)
        return RemoteDMATransfer(dst_ids=[DstId(rid=rid, pnc=pid)], dma_engine_mask=sum(1 << b for b in eng),
                                 remote_sem=rsem, src=in_, dst=out)

    def send(dst, out, in_, rsem, eng):
        rid, pid, _ = topo.addr(dst)
        sent[0] += len(eng)
        g.remote_dma(out, in_, rsem, sem.lsem, pid, rid, sum(1 << b for b in eng))

    if is_rank:
        other = part[ci][me] if is_host else host[ci][me]
        sy.dma_start(T.idx[0:16, 0:32], T.ex[:, :]).then_inc(sem.s_idx, 16)
        se.dma_start(T.idx[0:16, 32:64], T.pos[:, :]).then_inc(sem.s_idx, 16)
        sy.dma_start(T.xs[:, :], T.x[:, :]).then_inc(sem.s_x0, 16)
        se.dma_start(T.W[:, 0:WA], T.w1[:, 0:WA]).then_inc(sem.s_wa, 16)
        se.dma_start(T.W[:, 512:1024], T.w2[:, :]).then_inc(sem.s_w, 16)
        sy.dma_start(T.W[:, WA:512], T.w1[:, WA:512]).then_inc(sem.s_w, 16)
        g.iota(T.dv[0:16, :], [[0, 8], [1, 16]], 0, -1, allow_small_or_imprecise_dtypes=True).then_inc(sem.s_g, 1)
        g.iota(T.q[:, :], [[16, 32]], SLOTS, 1, allow_small_or_imprecise_dtypes=True).then_inc(sem.s_q, 1)
        ve.memset(T.S[:, 0:SLOTS], 0.0).then_inc(sem.s_set, 1)
        ve.wait_ge(sem.s_g, 1)
        for i, coef in enumerate((DROP, 12.0, 1.0, 180.0)):
            ve.tensor_scalar(T.repb[0:16, 128 * i:128 * i + 128], T.dv[0:16, :], 0.0, coef, Alu.is_equal, Alu.mult).then_inc(sem.s_cf, 1)
        ve.wait_ge(sem.s_idx, 32)
        ve.tensor_scalar(T.idx[0:16, 64:96], T.idx[0:16, 0:32], 3, None, Alu.bitwise_and).then_inc(sem.s_and, 1)
        ve.tensor_scalar(T.flb[0:16, 0:32], T.idx[0:16, 32:64], CAP, None, Alu.is_ge).then_inc(sem.s_f, 1)
        ve.wait_ge(sem.s_and, 1)
        ve.tensor_scalar(T.flb[0:16, 32:128], T.idx[0:16, 0:96], CAP, None, Alu.min).then_inc(sem.s_f, 1)
        te.wait_ge(sem.s_cf, 4)
        te.wait_ge(sem.s_f, 1)
        te.matmul(T.zp[:, 0:32], T.repb[0:16, 0:128], T.flb[0:16, 0:32], True, False)
        te.wait_ge(sem.s_f, 2)
        for i in range(1, 4):
            mm = te.matmul(T.zp[:, 0:32], T.repb[0:16, 128 * i:128 * i + 128], T.flb[0:16, 32 * i:32 * i + 32], False, i == 3)
        mm.then_inc(sem.s_z, 1)
        ve.wait_ge(sem.s_q, 1)
        ve.wait_ge(sem.s_z, 1)
        ve.tensor_tensor(T.zs[:, :], T.zp[:, 0:32], T.q[:, :], Alu.min).then_inc(sem.s_zs, 1)
        ve.wait_ge(sem.s_zs, 1)
        ve.tensor_copy(T.offs[:, :], T.zs[:, :]).then_inc(sem.s_off, 1)
        ve.wait_ge(sem.s_off, 1)
        ve.wait_ge(sem.s_set, 1)
        ve.wait_ge(sem.s_x0, 16)
        ve.tensor_copy(T.S[:, 0:WIN].indirect(T.offs[:, 0:32]), T.xs[:, :]).then_inc(sem.s_sc, 1)
        ve.tensor_scalar(T.offg[:, :], T.zp[:, 0:32], float(SLOTS), None, Alu.min).then_inc(sem.s_og, 1)
        ve.memset(T.R[:, SLOTS:SLOTS + 8], 0.0).then_inc(sem.s_og, 1)
        g.wait_ge(sem.s_wa, 16)
        send(other, T.W[:, 0:WA], T.W[:, 0:WA], sem.s_ws, bits(other))
        g.wait_ge(sem.s_sc, 1)
        g.remote_dma_fused([tr(host[ci][e], T.L[:, me, :, :], T.S[:, GRP * e:GRP * e + GRP], sem["p1_%d" % me],
                               bits(host[ci][e])[P1_ENG * e:P1_ENG * e + P1_ENG]) for e in range(NE) if host[ci][e] != core],
                           local_sem=sem.lsem)
        eng = bits(other)
        half = len(eng) // 2
        g.wait_ge(sem.s_w, 32)
        if is_host:
            send(other, T.W[:, WA:WA + 2 * WR], T.W[:, WA:WA + 2 * WR], sem.s_ws, home(other))
        else:
            g.remote_dma_fused([tr(other, T.W[:, WA:WA + WR], T.W[:, WA:WA + WR], sem.s_ws, eng[0:half]),
                                tr(other, T.W[:, WA + WR:WA + 2 * WR], T.W[:, WA + WR:WA + 2 * WR], sem.s_ws, eng[half:2 * half])],
                               local_sem=sem.lsem)

    n_m = n_ml = 0
    if is_host:
        if is_rank:
            ve.wait_ge(sem.s_sc, 1)
            for c in range(4):
                src = T.S[:, GRP * ex + CAP * c:GRP * ex + CAP * c + CAP]
                out = T.V[:, GRP * ci + CAP * me:GRP * ci + CAP * me + CAP] if c == ci else T.M[:, c, me, :]
                ve.tensor_copy(out, src).then_inc(sem.s_m, 1)
                n_m += 1
        for s in range(NE):
            if rc[ci][s] == core:
                continue
            ve.wait_ge(sem["p1_%d" % s], P1_ENG)
            ve.tensor_copy(T.M[:, :, s, :], T.L[:, s, :, :]).then_inc(sem.s_m, 1)
            n_m += 1
            se.wait_ge(sem["p1_%d" % s], P1_ENG)
            se.activation(T.V[:, GRP * ci + CAP * s:GRP * ci + CAP * s + CAP], T.L[:, s, ci, :], Act.Copy).then_inc(sem.s_ml, 1)
            n_ml += 1
        g.wait_ge(sem.s_m, n_m)
        for c in P["cross"][ci] + P["plane"][ci]:
            dst = host[c][ex] if c in P["cross"][ci] else part[c][ex]
            send(dst, T.V[:, GRP * ci:GRP * ci + GRP], T.M[:, c, :, :], sem["p2_%d" % ci], bits(dst)[0:OFF_ENG])

    pieces = []
    if is_host:
        pieces.append((ci, 0, NE, [(sem.s_m, n_m), (sem.s_ml, n_ml)]))
    for a in (P["take"][ci] if is_host else P["plane"][ci]):
        for s0, ns in cut(ci, a):
            pieces.append((a, s0, ns, [(sem["p2_%d" % a], OFF_ENG)]))
    if is_rank:
        te.wait_ge(sem.s_wa, 16)
        te.wait_ge(sem.s_w, 32)
    else:
        n_eng = len(bits(core, rc[ci][ex]))
        te.wait_ge(sem.s_ws, n_eng + (2 * (n_eng // 2) if is_host else len(home(core, rc[ci][ex]))))
    hp = [T.hp0, T.hp1, T.hp2, T.hp3]
    op = [T.op0, T.op1]
    for n, (c, s0, ns, waits) in enumerate(pieces):
        lo, w = GRP * c + CAP * s0, CAP * ns
        for s_, v_ in waits:
            te.wait_ge(s_, v_)
        for f in range(FF):
            te.matmul(hp[f][:, 0:w], T.W[:, 128 * f:128 * f + 128], T.V[:, lo:lo + w], True, True).then_inc(sem.s_l1, 1)
        for f in range(FF):
            hb = T.h[:, ((n % 2) * FF + f) * GRP:((n % 2) * FF + f) * GRP + w]
            eng = se if f % 2 == 0 else ve
            eng.wait_ge(sem.s_l1, FF * n + f + 1)
            if n >= 2:
                eng.wait_ge(sem.s_l2, FF * (n - 2) + f + 1)
            if f % 2 == 0:
                se.activation(hb, hp[f][:, 0:w], Act.Relu).then_inc(sem.s_ra, 1)
            else:
                ve.tensor_scalar(hb, hp[f][:, 0:w], 0.0, None, Alu.max).then_inc(sem.s_rv, 1)
        if n >= 2:
            te.wait_ge(sem.s_o, n - 1)
        for f in range(FF):
            hb = T.h[:, ((n % 2) * FF + f) * GRP:((n % 2) * FF + f) * GRP + w]
            te.wait_ge(sem.s_ra if f % 2 == 0 else sem.s_rv, 2 * n + f // 2 + 1)
            te.matmul(op[n % 2][:, 0:w], T.W[:, 512 + 128 * f:512 + 128 * f + 128], hb, f == 0, f == FF - 1).then_inc(sem.s_l2, 1)
        ve.wait_ge(sem.s_l2, FF * n + FF)
        ve.tensor_copy(T.OB[:, lo:lo + w], op[n % 2][:, 0:w]).then_inc(sem.s_o, 1)

    def rcol(e, x):
        return GRP * e + CAP * x

    n_self = [0]

    def deliver(buf, x, c, s0, ns, pick=bits):
        trs = []
        for s in range(s0, s0 + ns):
            src = buf[:, GRP * (x if c == ci else c) + CAP * s:GRP * (x if c == ci else c) + CAP * s + CAP]
            if rc[c][s] == core:
                ve.tensor_copy(T.R[:, rcol(ex, x):rcol(ex, x) + CAP], src).then_inc(sem.s_self, 1)
                n_self[0] += 1
            else:
                eng = pick(rc[c][s])
                wd = len(eng) // ns
                trs.append(tr(rc[c][s], T.R[:, rcol(ex, x):rcol(ex, x) + CAP], src, sem.r2, eng[wd * (s - s0):wd * (s - s0) + wd]))
        g.remote_dma_fused(trs, local_sem=sem.lsem)

    for n, (c, s0, ns, _) in enumerate(pieces):
        g.wait_ge(sem.s_o, n + 1)
        if c == ci:
            ve.wait_ge(sem.s_o, len(pieces))
            deliver(T.OB, ci, ci, s0, ns, home)
        elif len(cut(ci, c)) > 1:
            deliver(T.OB, ci, c, s0, ns)
        else:
            send(host[c][ex], T.RL[:, GRP * ci:GRP * ci + GRP], T.OB[:, GRP * c:GRP * c + GRP], sem["r1_%d" % ci],
                 bits(host[c][ex])[0:OFF_ENG])
    if is_host:
        for x in P["back"][ci]:
            if len(cut(x, ci)) == 1:
                g.wait_ge(sem["r1_%d" % x], OFF_ENG)
                if is_rank:
                    ve.wait_ge(sem["r1_%d" % x], OFF_ENG)
                deliver(T.RL, x, ci, 0, NE)

    if is_rank:
        total = 0
        for e in range(NE):
            for x in range(4):
                if x == ci or len(cut(x, ci)) == 1:
                    total += 0 if host[ci][e] == core else len((home if x == ci else bits)(core, host[ci][e])) // NE
                else:
                    frm = host[x][e] if ci in P["cross"][x] else part[x][e]
                    total += sum(len(bits(core, frm)) // ns for s0, ns in cut(x, ci) if s0 <= me < s0 + ns)
        for eng in (ve, se):
            eng.wait_ge(sem.r2, total)
            if n_self[0]:
                eng.wait_ge(sem.s_self, n_self[0])
            eng.wait_ge(sem.s_og, 2)
        ve.tensor_copy(T.ys[:, 0:256], T.R[:, 0:SLOTS + 8].indirect(T.offg[:, 0:16])).then_inc(sem.s_gv, 1)
        se.activation(T.ys[:, 256:512], T.R[:, 0:SLOTS + 8].indirect(T.offg[:, 16:32]), Act.Copy).then_inc(sem.s_ga, 1)
        sy.wait_ge(sem.s_gv, 1)
        sy.wait_ge(sem.s_ga, 1)
        sy.dma_start(T.y[:, :], T.ys[:, :]).then_inc(sem.s_y, 16)
        sy.wait_ge(sem.s_y, 16)
    if sent[0]:
        g.wait_ge(sem.lsem, sent[0])
